import numpy as np
import ml_dtypes


def mxq(x, axis, fmt="e4m3"):
    dtype, down = {"e4m3": (ml_dtypes.float8_e4m3fn, 7), "e5m2": (ml_dtypes.float8_e5m2, 14)}[fmt]
    v = np.moveaxis(np.asarray(x, np.float32).astype(ml_dtypes.bfloat16).astype(np.float64), axis, -1)
    blocks = v.reshape(v.shape[:-1] + (-1, 32))
    amax = np.abs(blocks).max(-1, keepdims=True)
    byte = np.maximum(np.where(amax > 0, np.frexp(amax)[1] - 1 + 127, 0) - down, 1)
    scale = np.exp2(byte - 127.0)
    codes = (blocks / scale).astype(np.float32).astype(dtype).astype(np.float64)
    return np.moveaxis((codes * scale).reshape(v.shape), -1, axis)


WIDE = False


def mx_kscale(k):
    if not WIDE:
        return np.ones(k)
    levels = np.array([10, -10, 5, -5, 0])
    if k % 512:
        return np.exp2(np.random.permutation(np.resize(levels, k // 32))).repeat(32)
    a = np.empty((k // 512, 16))
    for p in range(k // 512):
        a[p, :8] = np.random.permutation(np.resize(levels, 8))
        for g in range(8):
            far = levels[np.abs(levels - a[p, g]) >= 10]
            a[p, g + 8] = far[np.random.randint(len(far))]
    return np.exp2(a.ravel()).repeat(32)


def f64(x):
    return np.asarray(x).astype(np.float64)


def striped(idx):
    return np.tile(idx.reshape(-1, 16).T, (8, 1)).astype(np.uint16)


def unstriped(offs):
    return offs[:16].T.reshape(-1).astype(np.int64)


E2M1 = np.array([0.0, 0.5, 1.0, 1.5, 2.0, 3.0, 4.0, 6.0, -0.0, -0.5, -1.0, -1.5, -2.0, -3.0, -4.0, -6.0])


def pack_weight(w, fmt):
    k, n = w.shape
    w = f64(np.asarray(w, np.float32).astype(ml_dtypes.bfloat16)).reshape(k // 32, 32, n)
    amax = np.abs(w).max(1)
    if fmt == "e4m3":
        byte = np.frexp(amax)[1] - 1 + 127 - 7
    else:
        mant, ex = np.frexp(amax / 6.0)
        byte = np.where(mant > 0.5, ex, ex - 1) + 127
    byte = np.clip(np.where(amax > 0, byte, 1), 1, 254)
    scaled = (w * np.exp2(127.0 - byte)[:, None, :]).reshape(k, n).astype(np.float32)
    by_word = np.ascontiguousarray(scaled.reshape(k // 512, 128, 4, n).transpose(0, 1, 3, 2))
    if fmt == "e4m3":
        words = by_word.astype(ml_dtypes.float8_e4m3fn).view(np.uint8)
    else:
        c = by_word.astype(ml_dtypes.float4_e2m1fn).view(np.uint8) & 0xF
        words = (c[..., 0::2] | (c[..., 1::2] << 4)).reshape(k // 512, 128, 2 * n)
    return np.ascontiguousarray(words), np.ascontiguousarray(byte.astype(np.uint8).reshape(k // 512, 16, n))


def unpack_weight(words, scales, fmt):
    g, _, n = scales.shape
    words = np.ascontiguousarray(words).reshape(g, 128, n, -1)
    if fmt == "e4m3":
        vals = words.view(ml_dtypes.float8_e4m3fn).astype(np.float64)
    else:
        nib = np.empty((g, 128, n, 4), np.uint8)
        nib[..., 0::2] = words & 0xF
        nib[..., 1::2] = words >> 4
        vals = E2M1[nib]
    vals = vals * np.repeat(np.exp2(scales.astype(np.float64) - 127.0), 8, axis=1)[..., None]
    return vals.transpose(0, 1, 3, 2).reshape(g * 512, n)


def gelu(v):
    return 0.5 * v * (1.0 + np.tanh(np.sqrt(2.0 / np.pi) * (v + 0.044715 * v**3)))


K, H, N, T, S, P = 1024, 1024, 512, 4096, 1024, 512


def setup_inputs():
    n = np.random.standard_normal
    s = mx_kscale(K)[:, None]
    u = mx_kscale(H)[:, None]
    tab_words, tab_scales = pack_weight(n((K, T)) * s, "e4m3")
    w3_words, w3_scales = pack_weight(n((K, N)) / s / np.sqrt(K), "e2m1")
    perm = np.random.permutation(S)
    return {
        "tab_words": tab_words, "tab_scales": tab_scales,
        "offs": striped(np.random.permutation(T)[:S]),
        "pos1": striped(perm[:P]),
        "pos2": striped(perm[P:]),
        "w1": (0.7 * n((K, H)) / s / np.sqrt(K)).astype(np.float32),
        "temp": np.random.uniform(0.4, 1.6, H).astype(np.float32),
        "bias": (0.5 * n(H)).astype(np.float32),
        "mat": (0.4 * n((H, P))).astype(np.float32),
        "skip": np.random.uniform(0.6, 2.0, H).astype(np.float32),
        "wgs": np.exp(0.3 * n((128, P))).astype(np.float32),
        "gain": (np.random.uniform(0.5, 2.0, H) * u[:, 0]).astype(np.float32),
        "w2": (n((H, N)) / u / np.sqrt(H)).astype(np.float32),
        "w3_words": w3_words, "w3_scales": w3_scales,
        "base": (0.7 * n(N)).astype(np.float32),
    }


def reference(tab_words, tab_scales, offs, pos1, pos2, w1, temp, bias, mat, skip, wgs, gain, w2,
              w3_words, w3_scales, base):
    v = unpack_weight(tab_words, tab_scales, "e4m3")[:, unstriped(offs)]
    h = mxq(f64(w1), 0, "e4m3").T @ v
    look = np.exp(f64(temp)[:, None] * h[:, unstriped(pos1)] + f64(bias)[:, None])
    a = f64(mat) * look
    page = f64(skip)[:, None] * h
    page[:, unstriped(pos2)] = np.tile(f64(wgs), (H // 128, 1)) * a
    x = mxq(f64(gain)[:, None] * page, 0, "e4m3")
    y = mxq(f64(w2), 0, "e4m3").T @ x
    d = unpack_weight(w3_words, w3_scales, "e2m1").T @ v
    return y * d + f64(base)[:, None]

@@ -1,0 +1,305 @@
+from contextlib import ExitStack
+
+import concourse.mybir as mybir
+
+K, H, N, T, S, M = 1024, 1024, 512, 4096, 1024, 512
+FLOPS = 2 * K * H * S + 2 * H * N * S + 2 * K * N * S
+
+F32 = mybir.dt.float32
+BF16 = mybir.dt.bfloat16
+I32 = mybir.dt.int32
+U32 = mybir.dt.uint32
+U16 = mybir.dt.uint16
+U8 = mybir.dt.uint8
+FP8X4 = mybir.dt.float8_e4m3fn_x4
+FP4X4 = mybir.dt.float4_e2m1fn_x4
+MULT = mybir.AluOpType.mult
+ADD = mybir.AluOpType.add
+ACT = mybir.ActivationFunctionType
+
+P = 128
+HALF = 512
+
+
+def tile_list_silage_heating_readout_kernel(
+    tc, tab_words, tab_scales, offs, pos1, pos2, w1, temp, bias, mat, skip, wgs, gain, w2,
+    w3_words, w3_scales, base, out,
+):
+    nc = tc.nc
+    with ExitStack() as ctx:
+        sb = ctx.enter_context(tc.tile_pool(name="sb", bufs=1))
+        ps = ctx.enter_context(tc.psum_pool(name="ps", bufs=1))
+
+        def tile(name, shape, dtype, tag=None):
+            return sb.tile(shape, dtype, name=name, tag=tag or name, align_bytes=64)
+
+        def bank(name, number):
+            return ps.tile([P, HALF], F32, name=name, tag="bank%d" % number)
+
+        def load(name, shape, dtype, src, tag=None):
+            dst = tile(name, shape, dtype, tag)
+            nc.sync.dma_start(out=dst[:], in_=src)
+            return dst
+
+        def load_words(a):
+            dst = tile("tabw%d" % a, [P, T], U32)
+            nc.sync.dma_start(out=dst[:].bitcast(I32),
+                              in_=tab_words[a].rearrange("p t i -> p (t i)").bitcast(I32))
+            return dst
+
+        def load_weight(name, w, a, c0, c1, tag=None):
+            rows = w[512 * a:512 * (a + 1), c0:c1].rearrange("(p i) c -> p i c", i=4)
+            return load(name, [P, 4, c1 - c0], F32, rows, tag)
+
+        def load_rows(name, src, k, tag=None):
+            if k < 4:
+                rows = src[P * k:P * (k + 1), :]
+            else:
+                rows = src[512:1024, :].rearrange("(p t) m -> p t m", t=4)[:, k - 4, :]
+            return load(name, [P, M], F32, rows, tag)
+
+        def load_natural(name, vec):
+            with nc.allow_non_contiguous_dma(reason="one value a partition"):
+                return load(name, [P, 4], F32, vec[0:512].rearrange("(c p) -> p c", p=P))
+
+        def load_dealt(name, vec):
+            return load(name, [P, 4], F32, vec[512:1024].rearrange("(p t) -> p t", t=4))
+
+        def copy_on(engine, dst, src):
+            if engine == "scalar":
+                nc.scalar.copy(out=dst, in_=src)
+            else:
+                nc.vector.tensor_copy(out=dst, in_=src)
+
+        def interleave(engine, dst, src):
+            copy_on(engine, dst.rearrange("p (c j i) -> p c i j", i=4, j=4),
+                    src.rearrange("p i (c j) -> p c i j", j=4))
+
+        def quantize(codes, scales, grouped):
+            nc.vector.quantize_mx(out=codes.bitcast(FP8X4), scales=scales, in_=grouped)
+
+        def quantize_weight(name, raw, engine, pair=None, tag=None, codes_tag=None):
+            width = raw.shape[2] if pair is None else 2 * P
+            grouped = tile(name + "g", [P, 4 * width], BF16, tag)
+            if pair is not None:
+                copy_on(engine, grouped[:].rearrange("p (t q i) -> p q i t", t=2, i=4),
+                        raw[:].rearrange("p i (q t) -> p q i t", t=4)[:, :, :, 2 * pair:2 * pair + 2])
+            else:
+                interleave(engine, grouped[:], raw[:])
+            codes = tile(name + "c", [P, width], U32, codes_tag)
+            scales = tile(name + "s", [P, width], U8)
+            quantize(codes[:], scales[:], grouped[:])
+            return codes, scales
+
+        offs_sb = load("offs", [P, S // 16], U16, offs)
+        tabs = tile("tabs", [P, T], U8)
+        nc.vector.memset(tabs[:].bitcast(I32), 0)
+        tabw = [load_words(0)]
+        for q in range(4):
+            nc.sync.dma_start(out=tabs[32 * q:32 * q + 8, :].bitcast(I32),
+                              in_=tab_scales[:, 4 * q:4 * q + 4, :].bitcast(I32))
+        raw = {(0, 0): load_weight("w1r00", w1, 0, 0, 128)}
+        tabw.append(load_words(1))
+        raw[(0, 1)] = load_weight("w1r01", w1, 1, 0, 128)
+        temp_sb = [load_natural("temp0", temp)]
+        bias_sb = [load_natural("bias0", bias)]
+        pos1_sb = load("pos1", [P, M // 16], U16, pos1)
+        for a in range(2):
+            raw[(1, a)] = load_weight("w1r1%d" % a, w1, a, 128, 256)
+        wgs0 = load("wgs0", [P, M], F32, wgs)
+        mats = {0: load_rows("mat0", mat, 0)}
+        for a in range(2):
+            raw[(2, a)] = load_weight("w1r2%d" % a, w1, a, 256, 384)
+        skip_sb = [load_natural("skip0", skip)]
+        pos2_sb = load("pos2", [P, M // 16], U16, pos2)
+        mats[1] = load_rows("mat1", mat, 1)
+        for a in range(2):
+            raw[(3, a)] = load_weight("w1r3%d" % a, w1, a, 384, 512)
+        mats[2] = load_rows("mat2", mat, 2)
+        for a in range(2):
+            raw[(4, a)] = load_weight("w1r4%d" % a, w1, a, 512, 1024)
+        gain_sb = [load_natural("gain0", gain)]
+        mats[3] = load_rows("mat3", mat, 3)
+        temp_sb.append(load_dealt("temp1", temp))
+        bias_sb.append(load_dealt("bias1", bias))
+        skip_sb.append(load_dealt("skip1", skip))
+        gain_sb.append(load_dealt("gain1", gain))
+        wgs1 = tile("wgs1", [P, 4 * M], F32)
+        for q in range(4):
+            nc.sync.dma_start(out=wgs1[32 * q:32 * q + 32, :],
+                              in_=wgs.rearrange("(p t) m -> p (t m)", t=4))
+        mats[4] = load_rows("mat4", mat, 4, tag="w1r11")
+        w3s = tile("w3s", [P, 2 * N], U8)
+        nc.gpsimd.memset(w3s[:].bitcast(I32), 0)
+        vs1 = tile("vs1", [P, S], U8)
+        nc.gpsimd.memset(vs1[:].bitcast(I32), 0)
+        w3w = tile("w3w", [P, 2, 2 * N], U8)
+        nc.sync.dma_start(out=w3w[:].bitcast(I32), in_=w3_words.rearrange("a p c -> p a c").bitcast(I32))
+        for q in range(4):
+            nc.sync.dma_start(
+                out=w3s[32 * q:32 * q + 4, :].bitcast(I32).rearrange("r (a c) -> r a c", a=2),
+                in_=w3_scales[:, 4 * q:4 * q + 4, :].rearrange("a r c -> r a c").bitcast(I32))
+
+        vs = tile("vs", [P, S], U8)
+        nc.vector.tensor_copy(out=vs[:], in_=tabs[:].indirect(offs_sb[:]))
+        vw = [tile("vw0", [P, S], U32), tile("vw1", [P, S], U32)]
+        nc.vector.tensor_copy(out=vw[0][:], in_=tabw[0][:].indirect(offs_sb[:]))
+        w1q = {(0, 0): quantize_weight("w1q00", raw[(0, 0)], "scalar")}
+        nc.vector.tensor_copy(out=vw[1][:, 0:HALF], in_=tabw[1][:].indirect(offs_sb[:, 0:32]))
+        w1q[(0, 1)] = quantize_weight("w1q01", raw[(0, 1)], "scalar")
+        nc.vector.tensor_copy(out=vw[1][:, HALF:S], in_=tabw[1][:].indirect(offs_sb[:, 32:64]))
+        for q in range(4):
+            nc.sync.dma_start(out=vs1[32 * q:32 * q + 4, :].bitcast(I32),
+                              in_=vs[32 * q + 4:32 * q + 8, :].bitcast(I32))
+        mats[5] = load_rows("mat5", mat, 5, tag="w1r00")
+        w2raw = [load_weight("w2r0", w2, 0, 0, N)]
+        mats[6] = load_rows("mat6", mat, 6, tag="w1r01")
+        w2raw.append(load_weight("w2r1", w2, 1, 0, N))
+        mats[7] = load_rows("mat7", mat, 7, tag="w1r10")
+        base_sb = load_natural("base", base)
+
+        chunk_of = [(0, 0), (1, 0), (2, 0), (3, 0), (4, 0), (4, 128), (5, 0), (5, 128)]
+        xb = {}
+        page_tag = ["page0", "page1", "page2", "page1", "page2", "page1", "page2", "page1"]
+        h_tag = ["h0", "h1", "h2", "h3", "h4", "h5", "w1r40", "w1r41"]
+        prod_tag = ["prod0"] + h_tag
+        stage0 = tile("stage0", [P, 4, S], BF16)
+        pages = {}
+
+        def xb_slot(k):
+            if k < 4:
+                return tile("xb0_%d" % k, [P, S], BF16, tag=prod_tag[k + 1])[:]
+            if k == 4:
+                xb[1] = tile("xb1", [P, 4 * S], BF16, tag=prod_tag[5])
+            return xb[1][:, (k - 4) * S:(k - 3) * S]
+
+        def column(vectors, k):
+            return vectors[k // 4][:, k % 4:k % 4 + 1]
+
+        def row_tile(k):
+            chunk, c0 = chunk_of[k]
+            h = tile("h%d" % k, [P, S], F32, tag=h_tag[k])
+            accs = []
+            for half in range(2):
+                cols = slice(half * HALF, (half + 1) * HALF)
+                acc = bank("hacc%d_%d" % (k, half), 2 * (k % 2) + half)
+                for a in range(2):
+                    codes, scales = w1q[(chunk, a)]
+                    nc.tensor.matmul_mx(
+                        out=acc[:], lhsT=codes[:, c0:c0 + P].bitcast(FP8X4), lhsT_scale=scales[:, c0:c0 + P],
+                        rhs=vw[a][:, cols].bitcast(FP8X4), rhs_scale=vs[4 * a:P, cols],
+                        start=(a == 0), stop=(a == 1))
+                nc.scalar.copy(out=h[:, cols], in_=acc[:])
+                accs.append(acc)
+            look = tile("look%d" % k, [P, M], F32, tag="look%d" % k)[:]
+            prod = tile("prod%d" % k, [P, M], F32, tag=prod_tag[k])[:]
+            nc.scalar.activation(out=look, in_=h[:].indirect(pos1_sb[:]), func=ACT.Exp,
+                                 bias=column(bias_sb, k), scale=column(temp_sb, k))
+            mw = tile("mw%d" % k, [P, M], F32, tag="mw")[:]
+            wgs_rows = wgs0[:] if k < 4 else wgs1[:, (k - 4) * M:(k - 3) * M]
+            nc.gpsimd.tensor_tensor(out=mw, in0=mats[k][:], in1=wgs_rows, op=MULT)
+            nc.gpsimd.tensor_tensor(out=prod, in0=look, in1=mw, op=MULT)
+            page = tile("page%d" % k, [P, S], F32, tag=page_tag[k])
+            nc.vector.tensor_scalar(out=page[:], in0=h[:], scalar1=column(skip_sb, k), scalar2=None, op0=MULT)
+            nc.vector.tensor_copy(out=page[:].indirect(pos2_sb[:]), in_=prod)
+            pages[k] = page
+
+        def apply_gain(k, engine, cols=slice(0, S)):
+            slot = xb_slot(k)
+            dst, src = slot[:, cols], pages[k][:, cols]
+            if engine == "vector":
+                nc.vector.tensor_scalar(out=dst, in0=src, scalar1=column(gain_sb, k), scalar2=None, op0=MULT)
+            elif engine == "scalar":
+                nc.scalar.activation(out=dst, in_=src, func=ACT.Copy, scale=column(gain_sb, k))
+            else:
+                nc.gpsimd.tensor_scalar(out=dst, in0=src, scalar1=column(gain_sb, k), scalar2=0.0,
+                                        op0=MULT, op1=ADD)
+            if k < 4:
+                nc.sync.dma_start(out=stage0[32 * k:32 * k + 32, :, :], in_=slot)
+
+        d_sb = {}
+        d_all = tile("d", [P, 8, HALF], F32, tag="tabw0")
+
+        def readout_d(nt, half):
+            cols = slice(half * HALF, (half + 1) * HALF)
+            acc = bank("dacc%d_%d" % (nt, half), 4 * (1 - half) + nt)
+            for a in range(2):
+                v_scale = vs[:, cols] if a == 0 else vs1[:, cols]
+                nc.tensor.matmul_mx(
+                    out=acc[:], lhsT=w3w[:, a, 2 * P * nt:2 * P * (nt + 1)].bitcast(FP4X4),
+                    lhsT_scale=w3s[:, a * N + P * nt:a * N + P * (nt + 1)],
+                    rhs=vw[a][:, cols].bitcast(FP8X4), rhs_scale=v_scale,
+                    start=(a == 0), stop=(a == 1))
+            d = d_all[:, 4 * half + nt, :]
+            nc.scalar.copy(out=d, in_=acc[:])
+            d_sb[(nt, half)] = d
+
+        for a in range(2):
+            w1q[(1, a)] = quantize_weight("w1q1%d" % a, raw[(1, a)], "vector")
+        for a in range(2):
+            w1q[(2, a)] = quantize_weight("w1q2%d" % a, raw[(2, a)], "vector", tag=page_tag[0] if a else None)
+        row_tile(0)
+        for a in range(2):
+            w1q[(3, a)] = quantize_weight("w1q3%d" % a, raw[(3, a)], "scalar", tag=page_tag[1] if a else None)
+        row_tile(1)
+        apply_gain(0, "vector")
+        for a in range(2):
+            w1q[(4, a)] = quantize_weight("w1q4%d" % a, raw[(4, a)], "scalar", pair=0, tag=page_tag[2] if a else None)
+        row_tile(2)
+        apply_gain(1, "vector")
+        row_tile(3)
+        apply_gain(2, "vector")
+        for a in range(2):
+            w1q[(5, a)] = quantize_weight("w1q5%d" % a, raw[(4, a)], "scalar", pair=1)
+        row_tile(4)
+        apply_gain(3, "vector")
+        for nt in range(4):
+            readout_d(nt, 0)
+        row_tile(5)
+        apply_gain(4, "vector")
+        apply_gain(5, "vector")
+        w2q = [quantize_weight("w2q0", w2raw[0], "scalar")]
+        row_tile(6)
+        w2q.append(quantize_weight("w2q1", w2raw[1], "scalar"))
+        row_tile(7)
+        apply_gain(6, "vector")
+
+        xq = {}
+
+        def quantize_page(b, half, grouped):
+            xcodes = tile("xc%d_%d" % (b, half), [P, HALF], U32)
+            xscales = tile("xs%d_%d" % (b, half), [P, HALF], U8)
+            quantize(xcodes[:], xscales[:], grouped)
+            xq[(b, half)] = (xcodes, xscales)
+
+        for half in range(2):
+            cols = slice(half * HALF, (half + 1) * HALF)
+            grouped = tile("xg0_%d" % half, [P, 4 * HALF], BF16, tag=("look7", "mw")[half])
+            interleave("scalar", grouped[:], stage0[:, :, cols])
+            quantize_page(0, half, grouped[:])
+        xb1 = xb[1][:].rearrange("p (t j) -> p t j", t=4)
+        for half, engine in ((0, "vector"), (1, "scalar")):
+            cols = slice(half * HALF, (half + 1) * HALF)
+            apply_gain(7, engine, cols)
+            grouped = tile("xg1_%d" % half, [P, 4 * HALF], BF16, tag=("page0", "h5")[half])
+            interleave(engine, grouped[:], xb1[:, :, cols])
+            quantize_page(1, half, grouped[:])
+        for nt in range(4):
+            readout_d(nt, 1)
+        for half in range(2):
+            cols = slice(half * HALF, (half + 1) * HALF)
+            for nt in range(4):
+                acc = bank("yacc%d_%d" % (nt, half), 4 * (1 - half) + nt)
+                for b in range(2):
+                    codes, scales = w2q[b]
+                    xcodes, xscales = xq[(b, half)]
+                    nc.tensor.matmul_mx(
+                        out=acc[:], lhsT=codes[:, P * nt:P * (nt + 1)].bitcast(FP8X4),
+                        lhsT_scale=scales[:, P * nt:P * (nt + 1)],
+                        rhs=xcodes[:].bitcast(FP8X4), rhs_scale=xscales[:],
+                        start=(b == 0), stop=(b == 1))
+                d = d_sb[(nt, half)]
+                nc.vector.tensor_tensor(out=d, in0=acc[:], in1=d, op=MULT)
+                nc.gpsimd.tensor_scalar(out=d, in0=d, scalar1=1.0, scalar2=base_sb[:, nt:nt + 1],
+                                        op0=MULT, op1=ADD)
+                nc.sync.dma_start(out=out[P * nt:P * (nt + 1), cols], in_=d)

@@ -1,6 +1,7 @@
 from contextlib import ExitStack
 
 import concourse.mybir as mybir
+from concourse.masks import make_identity
 
 K, H, N, T, S, M = 1024, 1024, 512, 4096, 1024, 512
 FLOPS = 2 * K * H * S + 2 * H * N * S + 2 * K * N * S
@@ -58,12 +59,26 @@ def tile_list_silage_heating_readout_kernel(
                 rows = src[512:1024, :].rearrange("(p t) m -> p t m", t=4)[:, k - 4, :]
             return load(name, [P, M], F32, rows, tag)
 
-        def load_natural(name, vec):
-            with nc.allow_non_contiguous_dma(reason="one value a partition"):
-                return load(name, [P, 4], F32, vec[0:512].rearrange("(c p) -> p c", p=P))
+        def load_chunk(name, c0, c1):
+            dst = tile(name, [P, 2, 4, c1 - c0], F32)
+            for a in range(2):
+                nc.sync.dma_start(out=dst[:, a, :, :],
+                                  in_=w1[512 * a:512 * (a + 1), c0:c1].rearrange("(p i) c -> p i c", i=4))
+            return dst
 
-        def load_dealt(name, vec):
-            return load(name, [P, 4], F32, vec[512:1024].rearrange("(p t) -> p t", t=4))
+        def group_chunk(name, raw, tag=None):
+            grouped = tile(name + "g", [P, 8 * raw.shape[3]], BF16, tag)
+            nc.vector.tensor_copy(out=grouped[:].rearrange("p (a c j i) -> p a c i j", a=2, i=4, j=4),
+                                  in_=raw[:].rearrange("p a i (c j) -> p a c i j", j=4))
+            return grouped[:]
+
+        def by_pass(quantized):
+            codes, scales = quantized
+            width = codes.shape[1] // 2
+            return [(codes[:, a * width:(a + 1) * width], scales[:, a * width:(a + 1) * width]) for a in range(2)]
+
+        def load_small(dst, src):
+            nc.scalar.dma_start(out=dst, in_=src)
 
         def copy_on(engine, dst, src):
             if engine == "scalar":
@@ -71,115 +86,117 @@ def tile_list_silage_heating_readout_kernel(
             else:
                 nc.vector.tensor_copy(out=dst, in_=src)
 
+        def scale_on(engine, dst, src, factor):
+            if engine == "scalar":
+                nc.scalar.activation(out=dst, in_=src, func=ACT.Copy, scale=factor)
+            else:
+                nc.vector.tensor_scalar(out=dst, in0=src, scalar1=factor, scalar2=None, op0=MULT)
+
         def interleave(engine, dst, src):
             copy_on(engine, dst.rearrange("p (c j i) -> p c i j", i=4, j=4),
                     src.rearrange("p i (c j) -> p c i j", j=4))
 
-        def quantize(codes, scales, grouped):
-            nc.vector.quantize_mx(out=codes.bitcast(FP8X4), scales=scales, in_=grouped)
-
-        def quantize_weight(name, raw, engine, pair=None, tag=None, codes_tag=None):
-            width = raw.shape[2] if pair is None else 2 * P
-            grouped = tile(name + "g", [P, 4 * width], BF16, tag)
-            if pair is not None:
-                copy_on(engine, grouped[:].rearrange("p (t q i) -> p q i t", t=2, i=4),
-                        raw[:].rearrange("p i (q t) -> p q i t", t=4)[:, :, :, 2 * pair:2 * pair + 2])
-            else:
-                interleave(engine, grouped[:], raw[:])
-            codes = tile(name + "c", [P, width], U32, codes_tag)
+        def quantize(name, grouped, tag=None):
+            width = grouped.shape[1] // 4
+            codes = tile(name + "c", [P, width], U32, tag)
             scales = tile(name + "s", [P, width], U8)
-            quantize(codes[:], scales[:], grouped[:])
+            nc.vector.quantize_mx(out=codes[:].bitcast(FP8X4), scales=scales[:], in_=grouped)
             return codes, scales
 
-        offs_sb = load("offs", [P, S // 16], U16, offs)
+        def group_weight(name, raw, engine, dealt=False, tag=None):
+            grouped = tile(name + "g", [P, 4 * raw.shape[2]], BF16, tag)
+            if dealt:
+                copy_on(engine, grouped[:].rearrange("p (t q i) -> p q i t", t=4, i=4),
+                        raw[:].rearrange("p i (q t) -> p q i t", t=4))
+            else:
+                interleave(engine, grouped[:], raw[:])
+            return grouped[:]
+
         tabs = tile("tabs", [P, T], U8)
-        nc.vector.memset(tabs[:].bitcast(I32), 0)
+        nc.sync.dma_start(out=tabs[0:32, :].bitcast(I32),
+                          in_=tab_scales.rearrange("a q t -> q a t").bitcast(I32))
+        offs_sb = load("offs", [P, S // 16], U16, offs)
         tabw = [load_words(0)]
-        for q in range(4):
-            nc.sync.dma_start(out=tabs[32 * q:32 * q + 8, :].bitcast(I32),
-                              in_=tab_scales[:, 4 * q:4 * q + 4, :].bitcast(I32))
-        raw = {(0, 0): load_weight("w1r00", w1, 0, 0, 128)}
+        raw = {(0, a): load_weight("w1r0%d" % a, w1, a, 0, 128) for a in range(2)}
         tabw.append(load_words(1))
-        raw[(0, 1)] = load_weight("w1r01", w1, 1, 0, 128)
-        temp_sb = [load_natural("temp0", temp)]
-        bias_sb = [load_natural("bias0", bias)]
+        raw1 = load_chunk("w1r1", 128, 256)
         pos1_sb = load("pos1", [P, M // 16], U16, pos1)
-        for a in range(2):
-            raw[(1, a)] = load_weight("w1r1%d" % a, w1, a, 128, 256)
         wgs0 = load("wgs0", [P, M], F32, wgs)
-        mats = {0: load_rows("mat0", mat, 0)}
-        for a in range(2):
-            raw[(2, a)] = load_weight("w1r2%d" % a, w1, a, 256, 384)
-        skip_sb = [load_natural("skip0", skip)]
         pos2_sb = load("pos2", [P, M // 16], U16, pos2)
+        mats = {0: load_rows("mat0", mat, 0)}
+        raw[(3, 0)] = load_weight("w1r30", w1, 0, 512, 1024)
+        raw2 = load_chunk("w1r2", 256, 512)
         mats[1] = load_rows("mat1", mat, 1)
-        for a in range(2):
-            raw[(3, a)] = load_weight("w1r3%d" % a, w1, a, 384, 512)
+        raw[(3, 1)] = load_weight("w1r31", w1, 1, 512, 1024)
         mats[2] = load_rows("mat2", mat, 2)
-        for a in range(2):
-            raw[(4, a)] = load_weight("w1r4%d" % a, w1, a, 512, 1024)
-        gain_sb = [load_natural("gain0", gain)]
         mats[3] = load_rows("mat3", mat, 3)
-        temp_sb.append(load_dealt("temp1", temp))
-        bias_sb.append(load_dealt("bias1", bias))
-        skip_sb.append(load_dealt("skip1", skip))
-        gain_sb.append(load_dealt("gain1", gain))
         wgs1 = tile("wgs1", [P, 4 * M], F32)
-        for q in range(4):
+        for q in (0, 2, 1, 3):
             nc.sync.dma_start(out=wgs1[32 * q:32 * q + 32, :],
                               in_=wgs.rearrange("(p t) m -> p (t m)", t=4))
-        mats[4] = load_rows("mat4", mat, 4, tag="w1r11")
-        w3s = tile("w3s", [P, 2 * N], U8)
-        nc.gpsimd.memset(w3s[:].bitcast(I32), 0)
-        vs1 = tile("vs1", [P, S], U8)
-        nc.gpsimd.memset(vs1[:].bitcast(I32), 0)
+        mat1 = load("mat47", [P, 4, M], F32, mat[512:1024, :].rearrange("(p t) m -> p t m", t=4))
+        for t in range(4):
+            mats[4 + t] = mat1[:, t, :]
+        w2raw = [load_weight("w2r0", w2, 0, 0, N)]
+        w2raw.append(load_weight("w2r1", w2, 1, 0, N))
         w3w = tile("w3w", [P, 2, 2 * N], U8)
         nc.sync.dma_start(out=w3w[:].bitcast(I32), in_=w3_words.rearrange("a p c -> p a c").bitcast(I32))
+
+        vrows = tile("vrows", [P, P], F32)
+        nc.gpsimd.memset(vrows[:], 0.0)
+        for v, vec in enumerate((temp, bias, skip, gain, base)):
+            nc.gpsimd.dma_start(out=vrows[4 * v:4 * v + 4, :], in_=vec[0:512].rearrange("(c p) -> c p", p=P))
+        ident = tile("ident", [P, P], F32)
+        make_identity(nc, ident[:])
+        vs = tile("vs", [P, 2 * S], U8)
+        nc.vector.memset(vs[:].bitcast(I32), 0)
+        nc.vector.memset(tabs[32:64, :].bitcast(I32), 0)
+        nc.vector.memset(tabs[64:128, :].bitcast(I32), 0)
+        picked = tile("picked", [P, S], U8)
+        nc.vector.tensor_copy(out=picked[:], in_=tabs[:].indirect(offs_sb[:]))
         for q in range(4):
-            nc.sync.dma_start(
+            load_small(vs[32 * q:32 * q + 4, :].bitcast(I32).rearrange("r (a c) -> r a c", a=2),
+                       picked[8 * q:8 * q + 8, :].bitcast(I32))
+        vacc = bank("vacc", 7)
+        nc.tensor.transpose(vacc[:, 0:P], vrows[:], ident[:])
+        vcols0 = tile("vcols0", [P, 20], F32)
+        nc.scalar.copy(out=vcols0[:], in_=vacc[:, 0:20])
+
+        vcols1 = []
+        for v, vec in enumerate((temp, bias, skip, gain)):
+            vcols1.append(tile("vcols1_%d" % v, [P, 4], F32))
+            nc.gpsimd.dma_start(out=vcols1[v][:], in_=vec[512:1024].rearrange("(p t) -> p t", t=4))
+        w3s = tile("w3s", [P, 2 * N], U8)
+        nc.gpsimd.memset(w3s[:].bitcast(I32), 0)
+        for q in range(4):
+            nc.gpsimd.dma_start(
                 out=w3s[32 * q:32 * q + 4, :].bitcast(I32).rearrange("r (a c) -> r a c", a=2),
                 in_=w3_scales[:, 4 * q:4 * q + 4, :].rearrange("a r c -> r a c").bitcast(I32))
 
-        vs = tile("vs", [P, S], U8)
-        nc.vector.tensor_copy(out=vs[:], in_=tabs[:].indirect(offs_sb[:]))
+        TEMP, BIAS, SKIP, GAIN, BASE = range(5)
+
+        def column(v, k):
+            if k < 4:
+                return vcols0[:, 4 * v + k:4 * v + k + 1]
+            return vcols1[v][:, k - 4:k - 3]
+
         vw = [tile("vw0", [P, S], U32), tile("vw1", [P, S], U32)]
         nc.vector.tensor_copy(out=vw[0][:], in_=tabw[0][:].indirect(offs_sb[:]))
-        w1q = {(0, 0): quantize_weight("w1q00", raw[(0, 0)], "scalar")}
+        w1q = {}
+        for a in range(2):
+            w1q[(0, a)] = quantize("w1q0%d" % a, group_weight("w1q0%d" % a, raw[(0, a)], "vector"))
         nc.vector.tensor_copy(out=vw[1][:, 0:HALF], in_=tabw[1][:].indirect(offs_sb[:, 0:32]))
-        w1q[(0, 1)] = quantize_weight("w1q01", raw[(0, 1)], "scalar")
         nc.vector.tensor_copy(out=vw[1][:, HALF:S], in_=tabw[1][:].indirect(offs_sb[:, 32:64]))
-        for q in range(4):
-            nc.sync.dma_start(out=vs1[32 * q:32 * q + 4, :].bitcast(I32),
-                              in_=vs[32 * q + 4:32 * q + 8, :].bitcast(I32))
-        mats[5] = load_rows("mat5", mat, 5, tag="w1r00")
-        w2raw = [load_weight("w2r0", w2, 0, 0, N)]
-        mats[6] = load_rows("mat6", mat, 6, tag="w1r01")
-        w2raw.append(load_weight("w2r1", w2, 1, 0, N))
-        mats[7] = load_rows("mat7", mat, 7, tag="w1r10")
-        base_sb = load_natural("base", base)
 
-        chunk_of = [(0, 0), (1, 0), (2, 0), (3, 0), (4, 0), (4, 128), (5, 0), (5, 128)]
-        xb = {}
-        page_tag = ["page0", "page1", "page2", "page1", "page2", "page1", "page2", "page1"]
-        h_tag = ["h0", "h1", "h2", "h3", "h4", "h5", "w1r40", "w1r41"]
-        prod_tag = ["prod0"] + h_tag
-        stage0 = tile("stage0", [P, 4, S], BF16)
+        chunk_of = [(0, 0), (1, 0), (2, 0), (2, 128), (3, 0), (3, 128), (3, 256), (3, 384)]
+        stage0 = tile("stage0", [P, 4, S], BF16, tag="tabw1")
+        pairs1 = tile("pairs1", [P, 2, S, 2], BF16)
         pages = {}
+        looks = {}
 
-        def xb_slot(k):
-            if k < 4:
-                return tile("xb0_%d" % k, [P, S], BF16, tag=prod_tag[k + 1])[:]
-            if k == 4:
-                xb[1] = tile("xb1", [P, 4 * S], BF16, tag=prod_tag[5])
-            return xb[1][:, (k - 4) * S:(k - 3) * S]
-
-        def column(vectors, k):
-            return vectors[k // 4][:, k % 4:k % 4 + 1]
-
-        def row_tile(k):
+        def features(k, page_engine="scalar", tag=None, page_tag=None):
             chunk, c0 = chunk_of[k]
-            h = tile("h%d" % k, [P, S], F32, tag=h_tag[k])
-            accs = []
+            h = tile("h%d" % k, [P, S], F32, tag=tag or "h%d" % (k % 3))
             for half in range(2):
                 cols = slice(half * HALF, (half + 1) * HALF)
                 acc = bank("hacc%d_%d" % (k, half), 2 * (k % 2) + half)
@@ -187,109 +204,122 @@ def tile_list_silage_heating_readout_kernel(
                     codes, scales = w1q[(chunk, a)]
                     nc.tensor.matmul_mx(
                         out=acc[:], lhsT=codes[:, c0:c0 + P].bitcast(FP8X4), lhsT_scale=scales[:, c0:c0 + P],
-                        rhs=vw[a][:, cols].bitcast(FP8X4), rhs_scale=vs[4 * a:P, cols],
+                        rhs=vw[a][:, cols].bitcast(FP8X4), rhs_scale=vs[:, a * S + half * HALF:a * S + (half + 1) * HALF],
                         start=(a == 0), stop=(a == 1))
                 nc.scalar.copy(out=h[:, cols], in_=acc[:])
-                accs.append(acc)
-            look = tile("look%d" % k, [P, M], F32, tag="look%d" % k)[:]
-            prod = tile("prod%d" % k, [P, M], F32, tag=prod_tag[k])[:]
-            nc.scalar.activation(out=look, in_=h[:].indirect(pos1_sb[:]), func=ACT.Exp,
-                                 bias=column(bias_sb, k), scale=column(temp_sb, k))
-            mw = tile("mw%d" % k, [P, M], F32, tag="mw")[:]
-            wgs_rows = wgs0[:] if k < 4 else wgs1[:, (k - 4) * M:(k - 3) * M]
-            nc.gpsimd.tensor_tensor(out=mw, in0=mats[k][:], in1=wgs_rows, op=MULT)
-            nc.gpsimd.tensor_tensor(out=prod, in0=look, in1=mw, op=MULT)
-            page = tile("page%d" % k, [P, S], F32, tag=page_tag[k])
-            nc.vector.tensor_scalar(out=page[:], in0=h[:], scalar1=column(skip_sb, k), scalar2=None, op0=MULT)
-            nc.vector.tensor_copy(out=page[:].indirect(pos2_sb[:]), in_=prod)
-            pages[k] = page
+            looks[k] = tile("look%d" % k, [P, M], F32, tag="look%d" % k)
+            nc.scalar.activation(out=looks[k][:], in_=h[:].indirect(pos1_sb[:]), func=ACT.Exp,
+                                 bias=column(BIAS, k), scale=column(TEMP, k))
+            pages[k] = tile("page%d" % k, [P, S], F32, tag=page_tag or "page%d" % (k % 5))
+            scale_on(page_engine, pages[k][:], h[:], column(SKIP, k))
 
-        def apply_gain(k, engine, cols=slice(0, S)):
-            slot = xb_slot(k)
-            dst, src = slot[:, cols], pages[k][:, cols]
-            if engine == "vector":
-                nc.vector.tensor_scalar(out=dst, in0=src, scalar1=column(gain_sb, k), scalar2=None, op0=MULT)
-            elif engine == "scalar":
-                nc.scalar.activation(out=dst, in_=src, func=ACT.Copy, scale=column(gain_sb, k))
-            else:
-                nc.gpsimd.tensor_scalar(out=dst, in0=src, scalar1=column(gain_sb, k), scalar2=0.0,
-                                        op0=MULT, op1=ADD)
+        mws = {}
+
+        def weigh(k):
+            wgs_rows = wgs0[:] if k < 4 else wgs1[:, (k - 4) * M:(k - 3) * M]
+            mws[k] = tile("mw%d" % k, [P, M], F32, tag="page%d" % ((k - 2) % 5))
+            nc.vector.tensor_tensor(out=mws[k][:], in0=mats[k][:], in1=wgs_rows, op=MULT)
+
+        def put(k):
+            nc.vector.tensor_tensor(out=pages[k][:].indirect(pos2_sb[:]), in0=looks[k][:], in1=mws[k][:], op=MULT)
+
+        def apply_gain(k, engine):
             if k < 4:
-                nc.sync.dma_start(out=stage0[32 * k:32 * k + 32, :, :], in_=slot)
+                rounded = tile("rounded%d" % k, [P, S], BF16)
+                scale_on(engine, rounded[:], pages[k][:], column(GAIN, k))
+                nc.sync.dma_start(out=stage0[32 * k:32 * k + 32, :, :], in_=rounded[:])
+            else:
+                scale_on(engine, pairs1[:, (k - 4) // 2, :, k % 2], pages[k][:], column(GAIN, k))
 
         d_sb = {}
-        d_all = tile("d", [P, 8, HALF], F32, tag="tabw0")
 
         def readout_d(nt, half):
             cols = slice(half * HALF, (half + 1) * HALF)
-            acc = bank("dacc%d_%d" % (nt, half), 4 * (1 - half) + nt)
+            acc = bank("dacc%d_%d" % (nt, half), 4 + nt)
             for a in range(2):
-                v_scale = vs[:, cols] if a == 0 else vs1[:, cols]
                 nc.tensor.matmul_mx(
                     out=acc[:], lhsT=w3w[:, a, 2 * P * nt:2 * P * (nt + 1)].bitcast(FP4X4),
                     lhsT_scale=w3s[:, a * N + P * nt:a * N + P * (nt + 1)],
-                    rhs=vw[a][:, cols].bitcast(FP8X4), rhs_scale=v_scale,
+                    rhs=vw[a][:, cols].bitcast(FP8X4), rhs_scale=vs[:, a * S + half * HALF:a * S + (half + 1) * HALF],
                     start=(a == 0), stop=(a == 1))
-            d = d_all[:, 4 * half + nt, :]
-            nc.scalar.copy(out=d, in_=acc[:])
-            d_sb[(nt, half)] = d
-
-        for a in range(2):
-            w1q[(1, a)] = quantize_weight("w1q1%d" % a, raw[(1, a)], "vector")
-        for a in range(2):
-            w1q[(2, a)] = quantize_weight("w1q2%d" % a, raw[(2, a)], "vector", tag=page_tag[0] if a else None)
-        row_tile(0)
-        for a in range(2):
-            w1q[(3, a)] = quantize_weight("w1q3%d" % a, raw[(3, a)], "scalar", tag=page_tag[1] if a else None)
-        row_tile(1)
-        apply_gain(0, "vector")
-        for a in range(2):
-            w1q[(4, a)] = quantize_weight("w1q4%d" % a, raw[(4, a)], "scalar", pair=0, tag=page_tag[2] if a else None)
-        row_tile(2)
-        apply_gain(1, "vector")
-        row_tile(3)
-        apply_gain(2, "vector")
-        for a in range(2):
-            w1q[(5, a)] = quantize_weight("w1q5%d" % a, raw[(4, a)], "scalar", pair=1)
-        row_tile(4)
-        apply_gain(3, "vector")
-        for nt in range(4):
-            readout_d(nt, 0)
-        row_tile(5)
-        apply_gain(4, "vector")
-        apply_gain(5, "vector")
-        w2q = [quantize_weight("w2q0", w2raw[0], "scalar")]
-        row_tile(6)
-        w2q.append(quantize_weight("w2q1", w2raw[1], "scalar"))
-        row_tile(7)
-        apply_gain(6, "vector")
+            if nt == 0:
+                d_sb[half] = tile("d%d" % half, [P, 4, HALF], F32, tag="tabw%d" % (1 - half))
+            nc.scalar.copy(out=d_sb[half][:, nt, :], in_=acc[:])
 
         xq = {}
 
-        def quantize_page(b, half, grouped):
-            xcodes = tile("xc%d_%d" % (b, half), [P, HALF], U32)
-            xscales = tile("xs%d_%d" % (b, half), [P, HALF], U8)
-            quantize(xcodes[:], xscales[:], grouped)
-            xq[(b, half)] = (xcodes, xscales)
+        def regroup_block0(half, tag):
+            grouped = tile("xg0_%d" % half, [P, 4 * HALF], BF16, tag=tag)
+            interleave("scalar", grouped[:], stage0[:, :, half * HALF:(half + 1) * HALF])
+            xq[(0, half)] = quantize("x0_%d" % half, grouped[:])
 
-        for half in range(2):
-            cols = slice(half * HALF, (half + 1) * HALF)
-            grouped = tile("xg0_%d" % half, [P, 4 * HALF], BF16, tag=("look7", "mw")[half])
-            interleave("scalar", grouped[:], stage0[:, :, cols])
-            quantize_page(0, half, grouped[:])
-        xb1 = xb[1][:].rearrange("p (t j) -> p t j", t=4)
-        for half, engine in ((0, "vector"), (1, "scalar")):
-            cols = slice(half * HALF, (half + 1) * HALF)
-            apply_gain(7, engine, cols)
-            grouped = tile("xg1_%d" % half, [P, 4 * HALF], BF16, tag=("page0", "h5")[half])
-            interleave(engine, grouped[:], xb1[:, :, cols])
-            quantize_page(1, half, grouped[:])
+        def regroup_block1(half, engine, tag):
+            word = U32 if engine == "scalar" else I32
+            grouped = tile("xg1_%d" % half, [P, 4 * HALF], BF16, tag=tag)
+            words = pairs1[:].rearrange("p u j e -> p u (j e)").bitcast(word)[:, :, half * HALF:(half + 1) * HALF]
+            copy_on(engine, grouped[:].bitcast(word).rearrange("p (c i u) -> p c u i", i=4, u=2),
+                    words.rearrange("p u (c i) -> p c u i", i=4))
+            return grouped[:]
+
+        g1 = group_chunk("w1q1", raw1, tag="page0")
+        w1q[(1, 0)], w1q[(1, 1)] = by_pass(quantize("w1q1", g1))
+        weigh(0)
+        features(0, "vector")
+        put(0)
+        features(1)
+        g30 = group_weight("w1q30", raw[(3, 0)], "scalar", dealt=True)
+        g2 = group_chunk("w1q2", raw2)
+        w1q[(2, 0)], w1q[(2, 1)] = by_pass(quantize("w1q2", g2))
+        apply_gain(0, "scalar")
+        weigh(1)
+        put(1)
+        features(2, tag="w1r30")
+        w1q[(3, 0)] = quantize("w1q30", g30, tag="look1")
+        apply_gain(1, "vector")
+        g31 = group_weight("w1q31", raw[(3, 1)], "vector", dealt=True)
+        weigh(2)
+        w1q[(3, 1)] = quantize("w1q31", g31)
+        put(2)
+        features(3)
+        weigh(3)
+        apply_gain(2, "vector")
+        put(3)
+        features(4)
+        weigh(4)
+        g20 = group_weight("w2q0", w2raw[0], "scalar", tag="w1r2")
+        apply_gain(3, "vector")
+        put(4)
+        features(5)
+        weigh(5)
+        w2q = [quantize("w2q0", g20)]
+        apply_gain(4, "vector")
+        put(5)
+        features(6)
+        weigh(6)
+        g21 = group_weight("w2q1", w2raw[1], "scalar")
+        apply_gain(5, "vector")
+        w2q.append(quantize("w2q1", g21))
+        put(6)
+        weigh(7)
+        regroup_block0(0, "w1r31")
+        regroup_block0(1, "w1r30")
+        features(7, "vector", tag="tabw1")
+        apply_gain(6, "vector")
+        put(7)
         for nt in range(4):
+            readout_d(nt, 0)
+        for nt in range(3):
             readout_d(nt, 1)
+        apply_gain(7, "vector")
+        late = [regroup_block1(0, "vector", "w2r0"), regroup_block1(1, "scalar", "w2r1")]
+        for half in range(2):
+            xq[(1, half)] = quantize("x1_%d" % half, late[half])
+        readout_d(3, 1)
+        results = [tile("res0", [P, 4, HALF], F32, tag="w2r1"), tile("res1", [P, 4, HALF], F32, tag="mat47")]
         for half in range(2):
             cols = slice(half * HALF, (half + 1) * HALF)
             for nt in range(4):
-                acc = bank("yacc%d_%d" % (nt, half), 4 * (1 - half) + nt)
+                acc = bank("yacc%d_%d" % (nt, half), 4 * half + nt)
                 for b in range(2):
                     codes, scales = w2q[b]
                     xcodes, xscales = xq[(b, half)]
@@ -298,8 +328,12 @@ def tile_list_silage_heating_readout_kernel(
                         lhsT_scale=scales[:, P * nt:P * (nt + 1)],
                         rhs=xcodes[:].bitcast(FP8X4), rhs_scale=xscales[:],
                         start=(b == 0), stop=(b == 1))
-                d = d_sb[(nt, half)]
-                nc.vector.tensor_tensor(out=d, in0=acc[:], in1=d, op=MULT)
-                nc.gpsimd.tensor_scalar(out=d, in0=d, scalar1=1.0, scalar2=base_sb[:, nt:nt + 1],
-                                        op0=MULT, op1=ADD)
-                nc.sync.dma_start(out=out[P * nt:P * (nt + 1), cols], in_=d)
+                d = d_sb[half][:, nt, :]
+                res = results[half][:, nt, :]
+                nc.vector.tensor_tensor(out=res, in0=acc[:], in1=d, op=MULT)
+                if half == 0:
+                    nc.gpsimd.tensor_scalar(out=res, in0=res, scalar1=1.0, scalar2=column(BASE, nt),
+                                            op0=MULT, op1=ADD)
+                else:
+                    nc.scalar.activation(out=res, in_=res, func=ACT.Identity, bias=column(BASE, nt))
+                nc.sync.dma_start(out=out[P * nt:P * (nt + 1), cols], in_=res)

@@ -130,6 +130,10 @@ def tile_list_silage_heating_readout_kernel(
         raw[(3, 1)] = load_weight("w1r31", w1, 1, 512, 1024)
         mats[2] = load_rows("mat2", mat, 2)
         mats[3] = load_rows("mat3", mat, 3)
+        vcols1 = []
+        for v, vec in enumerate((temp, bias, skip, gain)):
+            vcols1.append(tile("vcols1_%d" % v, [P, 4], F32))
+            nc.sync.dma_start(out=vcols1[v][:], in_=vec[512:1024].rearrange("(p t) -> p t", t=4))
         wgs1 = tile("wgs1", [P, 4 * M], F32)
         for q in (0, 2, 1, 3):
             nc.sync.dma_start(out=wgs1[32 * q:32 * q + 32, :],
@@ -141,6 +145,12 @@ def tile_list_silage_heating_readout_kernel(
         w2raw.append(load_weight("w2r1", w2, 1, 0, N))
         w3w = tile("w3w", [P, 2, 2 * N], U8)
         nc.sync.dma_start(out=w3w[:].bitcast(I32), in_=w3_words.rearrange("a p c -> p a c").bitcast(I32))
+        w3s = tile("w3s", [P, 2 * N], U8)
+        nc.gpsimd.memset(w3s[:].bitcast(I32), 0)
+        for q in range(4):
+            nc.sync.dma_start(
+                out=w3s[32 * q:32 * q + 4, :].bitcast(I32).rearrange("r (a c) -> r a c", a=2),
+                in_=w3_scales[:, 4 * q:4 * q + 4, :].rearrange("a r c -> r a c").bitcast(I32))
 
         vrows = tile("vrows", [P, P], F32)
         nc.gpsimd.memset(vrows[:], 0.0)
@@ -162,16 +172,6 @@ def tile_list_silage_heating_readout_kernel(
         vcols0 = tile("vcols0", [P, 20], F32)
         nc.scalar.copy(out=vcols0[:], in_=vacc[:, 0:20])
 
-        vcols1 = []
-        for v, vec in enumerate((temp, bias, skip, gain)):
-            vcols1.append(tile("vcols1_%d" % v, [P, 4], F32))
-            nc.gpsimd.dma_start(out=vcols1[v][:], in_=vec[512:1024].rearrange("(p t) -> p t", t=4))
-        w3s = tile("w3s", [P, 2 * N], U8)
-        nc.gpsimd.memset(w3s[:].bitcast(I32), 0)
-        for q in range(4):
-            nc.gpsimd.dma_start(
-                out=w3s[32 * q:32 * q + 4, :].bitcast(I32).rearrange("r (a c) -> r a c", a=2),
-                in_=w3_scales[:, 4 * q:4 * q + 4, :].rearrange("a r c -> r a c").bitcast(I32))
 
         TEMP, BIAS, SKIP, GAIN, BASE = range(5)
 
@@ -186,7 +186,8 @@ def tile_list_silage_heating_readout_kernel(
         for a in range(2):
             w1q[(0, a)] = quantize("w1q0%d" % a, group_weight("w1q0%d" % a, raw[(0, a)], "vector"))
         nc.vector.tensor_copy(out=vw[1][:, 0:HALF], in_=tabw[1][:].indirect(offs_sb[:, 0:32]))
-        nc.vector.tensor_copy(out=vw[1][:, HALF:S], in_=tabw[1][:].indirect(offs_sb[:, 32:64]))
+        nc.vector.tensor_copy(out=vw[1][:, HALF:768], in_=tabw[1][:].indirect(offs_sb[:, 32:48]))
+        nc.vector.tensor_copy(out=vw[1][:, 768:S], in_=tabw[1][:].indirect(offs_sb[:, 48:64]))
 
         chunk_of = [(0, 0), (1, 0), (2, 0), (2, 128), (3, 0), (3, 128), (3, 256), (3, 384)]
         stage0 = tile("stage0", [P, 4, S], BF16, tag="tabw1")
@@ -197,16 +198,19 @@ def tile_list_silage_heating_readout_kernel(
         def features(k, page_engine="scalar", tag=None, page_tag=None):
             chunk, c0 = chunk_of[k]
             h = tile("h%d" % k, [P, S], F32, tag=tag or "h%d" % (k % 3))
-            for half in range(2):
-                cols = slice(half * HALF, (half + 1) * HALF)
-                acc = bank("hacc%d_%d" % (k, half), 2 * (k % 2) + half)
+            if k == 0:
+                pieces = [(0, HALF, 0), (HALF, 768, 1), (768, S, 4)]
+            else:
+                pieces = [(0, HALF, 2 * (k % 2)), (HALF, S, 2 * (k % 2) + 1)]
+            for j0, j1, number in pieces:
+                acc = bank("hacc%d_%d" % (k, j0), number)[:, 0:j1 - j0]
                 for a in range(2):
                     codes, scales = w1q[(chunk, a)]
                     nc.tensor.matmul_mx(
-                        out=acc[:], lhsT=codes[:, c0:c0 + P].bitcast(FP8X4), lhsT_scale=scales[:, c0:c0 + P],
-                        rhs=vw[a][:, cols].bitcast(FP8X4), rhs_scale=vs[:, a * S + half * HALF:a * S + (half + 1) * HALF],
+                        out=acc, lhsT=codes[:, c0:c0 + P].bitcast(FP8X4), lhsT_scale=scales[:, c0:c0 + P],
+                        rhs=vw[a][:, j0:j1].bitcast(FP8X4), rhs_scale=vs[:, a * S + j0:a * S + j1],
                         start=(a == 0), stop=(a == 1))
-                nc.scalar.copy(out=h[:, cols], in_=acc[:])
+                nc.scalar.copy(out=h[:, j0:j1], in_=acc)
             looks[k] = tile("look%d" % k, [P, M], F32, tag="look%d" % k)
             nc.scalar.activation(out=looks[k][:], in_=h[:].indirect(pos1_sb[:]), func=ACT.Exp,
                                  bias=column(BIAS, k), scale=column(TEMP, k))
@@ -308,13 +312,12 @@ def tile_list_silage_heating_readout_kernel(
         put(7)
         for nt in range(4):
             readout_d(nt, 0)
-        for nt in range(3):
+        for nt in range(4):
             readout_d(nt, 1)
         apply_gain(7, "vector")
         late = [regroup_block1(0, "vector", "w2r0"), regroup_block1(1, "scalar", "w2r1")]
         for half in range(2):
             xq[(1, half)] = quantize("x1_%d" % half, late[half])
-        readout_d(3, 1)
         results = [tile("res0", [P, 4, HALF], F32, tag="w2r1"), tile("res1", [P, 4, HALF], F32, tag="mat47")]
         for half in range(2):
             cols = slice(half * HALF, (half + 1) * HALF)
@@ -330,10 +333,20 @@ def tile_list_silage_heating_readout_kernel(
                         start=(b == 0), stop=(b == 1))
                 d = d_sb[half][:, nt, :]
                 res = results[half][:, nt, :]
-                nc.vector.tensor_tensor(out=res, in0=acc[:], in1=d, op=MULT)
-                if half == 0:
+                if (half, nt) in ():
+                    nc.scalar.copy(out=res, in_=acc[:])
+                    nc.gpsimd.tensor_tensor(out=res, in0=res, in1=d, op=MULT)
                     nc.gpsimd.tensor_scalar(out=res, in0=res, scalar1=1.0, scalar2=column(BASE, nt),
                                             op0=MULT, op1=ADD)
-                else:
-                    nc.scalar.activation(out=res, in_=res, func=ACT.Identity, bias=column(BASE, nt))
-                nc.sync.dma_start(out=out[P * nt:P * (nt + 1), cols], in_=res)
+                    nc.sync.dma_start(out=out[P * nt:P * (nt + 1), cols], in_=res)
+                    continue
+                for j0, j1 in (((0, 256), (256, HALF)) if (half, nt) == (1, 3) else ((0, HALF),)):
+                    nc.vector.tensor_tensor(out=res[:, j0:j1], in0=acc[:, j0:j1], in1=d[:, j0:j1], op=MULT)
+                    if (half, nt) in ():
+                        nc.gpsimd.tensor_scalar(out=res[:, j0:j1], in0=res[:, j0:j1], scalar1=1.0,
+                                                scalar2=column(BASE, nt), op0=MULT, op1=ADD)
+                    else:
+                        nc.scalar.activation(out=res[:, j0:j1], in_=res[:, j0:j1], func=ACT.Identity,
+                                             bias=column(BASE, nt))
+                    nc.sync.dma_start(out=out[P * nt:P * (nt + 1), half * HALF + j0:half * HALF + j1],
+                                      in_=res[:, j0:j1])

from contextlib import ExitStack

import concourse.mybir as mybir
from concourse.masks import make_identity

K, H, N, T, S, M = 1024, 1024, 512, 4096, 1024, 512
FLOPS = 2 * K * H * S + 2 * H * N * S + 2 * K * N * S

F32 = mybir.dt.float32
BF16 = mybir.dt.bfloat16
I32 = mybir.dt.int32
U32 = mybir.dt.uint32
U16 = mybir.dt.uint16
U8 = mybir.dt.uint8
FP8X4 = mybir.dt.float8_e4m3fn_x4
FP4X4 = mybir.dt.float4_e2m1fn_x4
MULT = mybir.AluOpType.mult
ADD = mybir.AluOpType.add
ACT = mybir.ActivationFunctionType

P = 128
HALF = 512


def tile_list_silage_heating_readout_kernel(
    tc, tab_words, tab_scales, offs, pos1, pos2, w1, temp, bias, mat, skip, wgs, gain, w2,
    w3_words, w3_scales, base, out,
):
    nc = tc.nc
    with ExitStack() as ctx:
        sb = ctx.enter_context(tc.tile_pool(name="sb", bufs=1))
        ps = ctx.enter_context(tc.psum_pool(name="ps", bufs=1))

        def tile(name, shape, dtype, tag=None):
            return sb.tile(shape, dtype, name=name, tag=tag or name, align_bytes=64)

        def bank(name, number):
            return ps.tile([P, HALF], F32, name=name, tag="bank%d" % number)

        def load(name, shape, dtype, src, tag=None):
            dst = tile(name, shape, dtype, tag)
            nc.sync.dma_start(out=dst[:], in_=src)
            return dst

        def load_words(a):
            dst = tile("tabw%d" % a, [P, T], U32)
            nc.sync.dma_start(out=dst[:].bitcast(I32),
                              in_=tab_words[a].rearrange("p t i -> p (t i)").bitcast(I32))
            return dst

        def load_weight(name, w, a, c0, c1, tag=None):
            rows = w[512 * a:512 * (a + 1), c0:c1].rearrange("(p i) c -> p i c", i=4)
            return load(name, [P, 4, c1 - c0], F32, rows, tag)

        def load_rows(name, src, k, tag=None):
            if k < 4:
                rows = src[P * k:P * (k + 1), :]
            else:
                rows = src[512:1024, :].rearrange("(p t) m -> p t m", t=4)[:, k - 4, :]
            return load(name, [P, M], F32, rows, tag)

        def load_chunk(name, c0, c1):
            dst = tile(name, [P, 2, 4, c1 - c0], F32)
            for a in range(2):
                nc.sync.dma_start(out=dst[:, a, :, :],
                                  in_=w1[512 * a:512 * (a + 1), c0:c1].rearrange("(p i) c -> p i c", i=4))
            return dst

        def group_chunk(name, raw, tag=None):
            grouped = tile(name + "g", [P, 8 * raw.shape[3]], BF16, tag)
            nc.vector.tensor_copy(out=grouped[:].rearrange("p (a c j i) -> p a c i j", a=2, i=4, j=4),
                                  in_=raw[:].rearrange("p a i (c j) -> p a c i j", j=4))
            return grouped[:]

        def by_pass(quantized):
            codes, scales = quantized
            width = codes.shape[1] // 2
            return [(codes[:, a * width:(a + 1) * width], scales[:, a * width:(a + 1) * width]) for a in range(2)]

        def load_small(dst, src):
            nc.scalar.dma_start(out=dst, in_=src)

        def copy_on(engine, dst, src):
            if engine == "scalar":
                nc.scalar.copy(out=dst, in_=src)
            else:
                nc.vector.tensor_copy(out=dst, in_=src)

        def scale_on(engine, dst, src, factor):
            if engine == "scalar":
                nc.scalar.activation(out=dst, in_=src, func=ACT.Copy, scale=factor)
            else:
                nc.vector.tensor_scalar(out=dst, in0=src, scalar1=factor, scalar2=None, op0=MULT)

        def interleave(engine, dst, src):
            copy_on(engine, dst.rearrange("p (c j i) -> p c i j", i=4, j=4),
                    src.rearrange("p i (c j) -> p c i j", j=4))

        def quantize(name, grouped, tag=None):
            width = grouped.shape[1] // 4
            codes = tile(name + "c", [P, width], U32, tag)
            scales = tile(name + "s", [P, width], U8)
            nc.vector.quantize_mx(out=codes[:].bitcast(FP8X4), scales=scales[:], in_=grouped)
            return codes, scales

        def group_weight(name, raw, engine, dealt=False, tag=None):
            grouped = tile(name + "g", [P, 4 * raw.shape[2]], BF16, tag)
            if dealt:
                copy_on(engine, grouped[:].rearrange("p (t q i) -> p q i t", t=4, i=4),
                        raw[:].rearrange("p i (q t) -> p q i t", t=4))
            else:
                interleave(engine, grouped[:], raw[:])
            return grouped[:]

        tabs = tile("tabs", [P, T], U8)
        nc.sync.dma_start(out=tabs[0:32, :].bitcast(I32),
                          in_=tab_scales.rearrange("a q t -> q a t").bitcast(I32))
        offs_sb = load("offs", [P, S // 16], U16, offs)
        tabw = [load_words(0)]
        raw = {(0, a): load_weight("w1r0%d" % a, w1, a, 0, 128) for a in range(2)}
        tabw.append(load_words(1))
        raw1 = load_chunk("w1r1", 128, 256)
        pos1_sb = load("pos1", [P, M // 16], U16, pos1)
        wgs0 = load("wgs0", [P, M], F32, wgs)
        pos2_sb = load("pos2", [P, M // 16], U16, pos2)
        mats = {0: load_rows("mat0", mat, 0)}
        raw[(3, 0)] = load_weight("w1r30", w1, 0, 512, 1024)
        raw2 = load_chunk("w1r2", 256, 512)
        mats[1] = load_rows("mat1", mat, 1)
        raw[(3, 1)] = load_weight("w1r31", w1, 1, 512, 1024)
        mats[2] = load_rows("mat2", mat, 2)
        mats[3] = load_rows("mat3", mat, 3)
        vcols1 = []
        for v, vec in enumerate((temp, bias, skip, gain)):
            vcols1.append(tile("vcols1_%d" % v, [P, 4], F32))
            nc.sync.dma_start(out=vcols1[v][:], in_=vec[512:1024].rearrange("(p t) -> p t", t=4))
        wgs1 = tile("wgs1", [P, 4 * M], F32)
        for q in (0, 2, 1, 3):
            nc.sync.dma_start(out=wgs1[32 * q:32 * q + 32, :],
                              in_=wgs.rearrange("(p t) m -> p (t m)", t=4))
        mat1 = load("mat47", [P, 4, M], F32, mat[512:1024, :].rearrange("(p t) m -> p t m", t=4))
        for t in range(4):
            mats[4 + t] = mat1[:, t, :]
        w2raw = [load_weight("w2r0", w2, 0, 0, N)]
        w2raw.append(load_weight("w2r1", w2, 1, 0, N))
        w3w = tile("w3w", [P, 2, 2 * N], U8)
        nc.sync.dma_start(out=w3w[:].bitcast(I32), in_=w3_words.rearrange("a p c -> p a c").bitcast(I32))
        w3s = tile("w3s", [P, 2 * N], U8)
        nc.gpsimd.memset(w3s[:].bitcast(I32), 0)
        for q in range(4):
            nc.sync.dma_start(
                out=w3s[32 * q:32 * q + 4, :].bitcast(I32).rearrange("r (a c) -> r a c", a=2),
                in_=w3_scales[:, 4 * q:4 * q + 4, :].rearrange("a r c -> r a c").bitcast(I32))

        vrows = tile("vrows", [P, P], F32)
        nc.gpsimd.memset(vrows[:], 0.0)
        for v, vec in enumerate((temp, bias, skip, gain, base)):
            nc.gpsimd.dma_start(out=vrows[4 * v:4 * v + 4, :], in_=vec[0:512].rearrange("(c p) -> c p", p=P))
        ident = tile("ident", [P, P], F32)
        make_identity(nc, ident[:])
        vs = tile("vs", [P, 2 * S], U8)
        nc.vector.memset(vs[:].bitcast(I32), 0)
        nc.vector.memset(tabs[32:64, :].bitcast(I32), 0)
        nc.vector.memset(tabs[64:128, :].bitcast(I32), 0)
        picked = tile("picked", [P, S], U8)
        nc.vector.tensor_copy(out=picked[:], in_=tabs[:].indirect(offs_sb[:]))
        for q in range(4):
            load_small(vs[32 * q:32 * q + 4, :].bitcast(I32).rearrange("r (a c) -> r a c", a=2),
                       picked[8 * q:8 * q + 8, :].bitcast(I32))
        vacc = bank("vacc", 7)
        nc.tensor.transpose(vacc[:, 0:P], vrows[:], ident[:])
        vcols0 = tile("vcols0", [P, 20], F32)
        nc.scalar.copy(out=vcols0[:], in_=vacc[:, 0:20])


        TEMP, BIAS, SKIP, GAIN, BASE = range(5)

        def column(v, k):
            if k < 4:
                return vcols0[:, 4 * v + k:4 * v + k + 1]
            return vcols1[v][:, k - 4:k - 3]

        vw = [tile("vw0", [P, S], U32), tile("vw1", [P, S], U32)]
        nc.vector.tensor_copy(out=vw[0][:], in_=tabw[0][:].indirect(offs_sb[:]))
        w1q = {}
        for a in range(2):
            w1q[(0, a)] = quantize("w1q0%d" % a, group_weight("w1q0%d" % a, raw[(0, a)], "vector"))
        nc.vector.tensor_copy(out=vw[1][:, 0:HALF], in_=tabw[1][:].indirect(offs_sb[:, 0:32]))
        nc.vector.tensor_copy(out=vw[1][:, HALF:768], in_=tabw[1][:].indirect(offs_sb[:, 32:48]))
        nc.vector.tensor_copy(out=vw[1][:, 768:S], in_=tabw[1][:].indirect(offs_sb[:, 48:64]))

        chunk_of = [(0, 0), (1, 0), (2, 0), (2, 128), (3, 0), (3, 128), (3, 256), (3, 384)]
        stage0 = tile("stage0", [P, 4, S], BF16, tag="tabw1")
        pairs1 = tile("pairs1", [P, 2, S, 2], BF16)
        pages = {}
        looks = {}

        def features(k, page_engine="scalar", tag=None, page_tag=None):
            chunk, c0 = chunk_of[k]
            h = tile("h%d" % k, [P, S], F32, tag=tag or "h%d" % (k % 3))
            if k == 0:
                pieces = [(0, HALF, 0), (HALF, 768, 1), (768, S, 4)]
            else:
                pieces = [(0, HALF, 2 * (k % 2)), (HALF, S, 2 * (k % 2) + 1)]
            for j0, j1, number in pieces:
                acc = bank("hacc%d_%d" % (k, j0), number)[:, 0:j1 - j0]
                for a in range(2):
                    codes, scales = w1q[(chunk, a)]
                    nc.tensor.matmul_mx(
                        out=acc, lhsT=codes[:, c0:c0 + P].bitcast(FP8X4), lhsT_scale=scales[:, c0:c0 + P],
                        rhs=vw[a][:, j0:j1].bitcast(FP8X4), rhs_scale=vs[:, a * S + j0:a * S + j1],
                        start=(a == 0), stop=(a == 1))
                nc.scalar.copy(out=h[:, j0:j1], in_=acc)
            looks[k] = tile("look%d" % k, [P, M], F32, tag="look%d" % k)
            nc.scalar.activation(out=looks[k][:], in_=h[:].indirect(pos1_sb[:]), func=ACT.Exp,
                                 bias=column(BIAS, k), scale=column(TEMP, k))
            pages[k] = tile("page%d" % k, [P, S], F32, tag=page_tag or "page%d" % (k % 5))
            scale_on(page_engine, pages[k][:], h[:], column(SKIP, k))

        mws = {}

        def weigh(k):
            wgs_rows = wgs0[:] if k < 4 else wgs1[:, (k - 4) * M:(k - 3) * M]
            mws[k] = tile("mw%d" % k, [P, M], F32, tag="page%d" % ((k - 2) % 5))
            nc.vector.tensor_tensor(out=mws[k][:], in0=mats[k][:], in1=wgs_rows, op=MULT)

        def put(k):
            nc.vector.tensor_tensor(out=pages[k][:].indirect(pos2_sb[:]), in0=looks[k][:], in1=mws[k][:], op=MULT)

        def apply_gain(k, engine):
            if k < 4:
                rounded = tile("rounded%d" % k, [P, S], BF16)
                scale_on(engine, rounded[:], pages[k][:], column(GAIN, k))
                nc.sync.dma_start(out=stage0[32 * k:32 * k + 32, :, :], in_=rounded[:])
            else:
                scale_on(engine, pairs1[:, (k - 4) // 2, :, k % 2], pages[k][:], column(GAIN, k))

        d_sb = {}

        def readout_d(nt, half):
            cols = slice(half * HALF, (half + 1) * HALF)
            acc = bank("dacc%d_%d" % (nt, half), 4 + nt)
            for a in range(2):
                nc.tensor.matmul_mx(
                    out=acc[:], lhsT=w3w[:, a, 2 * P * nt:2 * P * (nt + 1)].bitcast(FP4X4),
                    lhsT_scale=w3s[:, a * N + P * nt:a * N + P * (nt + 1)],
                    rhs=vw[a][:, cols].bitcast(FP8X4), rhs_scale=vs[:, a * S + half * HALF:a * S + (half + 1) * HALF],
                    start=(a == 0), stop=(a == 1))
            if nt == 0:
                d_sb[half] = tile("d%d" % half, [P, 4, HALF], F32, tag="tabw%d" % (1 - half))
            nc.scalar.copy(out=d_sb[half][:, nt, :], in_=acc[:])

        xq = {}

        def regroup_block0(half, tag):
            grouped = tile("xg0_%d" % half, [P, 4 * HALF], BF16, tag=tag)
            interleave("scalar", grouped[:], stage0[:, :, half * HALF:(half + 1) * HALF])
            xq[(0, half)] = quantize("x0_%d" % half, grouped[:])

        def regroup_block1(half, engine, tag):
            word = U32 if engine == "scalar" else I32
            grouped = tile("xg1_%d" % half, [P, 4 * HALF], BF16, tag=tag)
            words = pairs1[:].rearrange("p u j e -> p u (j e)").bitcast(word)[:, :, half * HALF:(half + 1) * HALF]
            copy_on(engine, grouped[:].bitcast(word).rearrange("p (c i u) -> p c u i", i=4, u=2),
                    words.rearrange("p u (c i) -> p c u i", i=4))
            return grouped[:]

        g1 = group_chunk("w1q1", raw1, tag="page0")
        w1q[(1, 0)], w1q[(1, 1)] = by_pass(quantize("w1q1", g1))
        weigh(0)
        features(0, "vector")
        put(0)
        features(1)
        g30 = group_weight("w1q30", raw[(3, 0)], "scalar", dealt=True)
        g2 = group_chunk("w1q2", raw2)
        w1q[(2, 0)], w1q[(2, 1)] = by_pass(quantize("w1q2", g2))
        apply_gain(0, "scalar")
        weigh(1)
        put(1)
        features(2, tag="w1r30")
        w1q[(3, 0)] = quantize("w1q30", g30, tag="look1")
        apply_gain(1, "vector")
        g31 = group_weight("w1q31", raw[(3, 1)], "vector", dealt=True)
        weigh(2)
        w1q[(3, 1)] = quantize("w1q31", g31)
        put(2)
        features(3)
        weigh(3)
        apply_gain(2, "vector")
        put(3)
        features(4)
        weigh(4)
        g20 = group_weight("w2q0", w2raw[0], "scalar", tag="w1r2")
        apply_gain(3, "vector")
        put(4)
        features(5)
        weigh(5)
        w2q = [quantize("w2q0", g20)]
        apply_gain(4, "vector")
        put(5)
        features(6)
        weigh(6)
        g21 = group_weight("w2q1", w2raw[1], "scalar")
        apply_gain(5, "vector")
        w2q.append(quantize("w2q1", g21))
        put(6)
        weigh(7)
        regroup_block0(0, "w1r31")
        regroup_block0(1, "w1r30")
        features(7, "vector", tag="tabw1")
        apply_gain(6, "vector")
        put(7)
        for nt in range(4):
            readout_d(nt, 0)
        for nt in range(4):
            readout_d(nt, 1)
        apply_gain(7, "vector")
        late = [regroup_block1(0, "vector", "w2r0"), regroup_block1(1, "scalar", "w2r1")]
        for half in range(2):
            xq[(1, half)] = quantize("x1_%d" % half, late[half])
        results = [tile("res0", [P, 4, HALF], F32, tag="w2r1"), tile("res1", [P, 4, HALF], F32, tag="mat47")]
        for half in range(2):
            cols = slice(half * HALF, (half + 1) * HALF)
            for nt in range(4):
                acc = bank("yacc%d_%d" % (nt, half), 4 * half + nt)
                for b in range(2):
                    codes, scales = w2q[b]
                    xcodes, xscales = xq[(b, half)]
                    nc.tensor.matmul_mx(
                        out=acc[:], lhsT=codes[:, P * nt:P * (nt + 1)].bitcast(FP8X4),
                        lhsT_scale=scales[:, P * nt:P * (nt + 1)],
                        rhs=xcodes[:].bitcast(FP8X4), rhs_scale=xscales[:],
                        start=(b == 0), stop=(b == 1))
                d = d_sb[half][:, nt, :]
                res = results[half][:, nt, :]
                if (half, nt) in ():
                    nc.scalar.copy(out=res, in_=acc[:])
                    nc.gpsimd.tensor_tensor(out=res, in0=res, in1=d, op=MULT)
                    nc.gpsimd.tensor_scalar(out=res, in0=res, scalar1=1.0, scalar2=column(BASE, nt),
                                            op0=MULT, op1=ADD)
                    nc.sync.dma_start(out=out[P * nt:P * (nt + 1), cols], in_=res)
                    continue
                for j0, j1 in (((0, 256), (256, HALF)) if (half, nt) == (1, 3) else ((0, HALF),)):
                    nc.vector.tensor_tensor(out=res[:, j0:j1], in0=acc[:, j0:j1], in1=d[:, j0:j1], op=MULT)
                    if (half, nt) in ():
                        nc.gpsimd.tensor_scalar(out=res[:, j0:j1], in0=res[:, j0:j1], scalar1=1.0,
                                                scalar2=column(BASE, nt), op0=MULT, op1=ADD)
                    else:
                        nc.scalar.activation(out=res[:, j0:j1], in_=res[:, j0:j1], func=ACT.Identity,
                                             bias=column(BASE, nt))
                    nc.sync.dma_start(out=out[P * nt:P * (nt + 1), half * HALF + j0:half * HALF + j1],
                                      in_=res[:, j0:j1])
